import numpy as np
import ml_dtypes


def mxq(x, axis, fmt="e4m3"):
    dtype, down = {"e4m3": (ml_dtypes.float8_e4m3fn, 7), "e5m2": (ml_dtypes.float8_e5m2, 14)}[fmt]
    v = np.moveaxis(np.asarray(x, np.float32).astype(ml_dtypes.bfloat16).astype(np.float64), axis, -1)
    blocks = v.reshape(v.shape[:-1] + (-1, 32))
    amax = np.abs(blocks).max(-1, keepdims=True)
    byte = np.maximum(np.where(amax > 0, np.frexp(amax)[1] - 1 + 127, 0) - down, 1)
    scale = np.exp2(byte - 127.0)
    codes = (blocks / scale).astype(np.float32).astype(dtype).astype(np.float64)
    return np.moveaxis((codes * scale).reshape(v.shape), -1, axis)


WIDE = False


def mx_kscale(k, group=512):
    if not WIDE:
        return np.ones(k)
    levels = np.array([18, -18])
    if group != 512:
        return np.exp2(np.random.permutation(np.resize(levels, k // group))).repeat(group)
    if k % 512:
        return np.exp2(np.random.permutation(np.resize(levels, k // 32))).repeat(32)
    a = np.empty((k // 512, 16))
    for p in range(k // 512):
        a[p, :8] = np.random.permutation(np.resize(levels, 8))
        for g in range(8):
            far = levels[np.abs(levels - a[p, g]) >= 10]
            a[p, g + 8] = far[np.random.randint(len(far))]
    return np.exp2(a.ravel()).repeat(32)


def f64(x):
    return np.asarray(x).astype(np.float64)


def sigmoid(v):
    return 1.0 / (1.0 + np.exp(-v))


G, D, M, O, N = 4, 128, 128, 128, 512


def setup_inputs():
    n = np.random.standard_normal
    s_d = mx_kscale(D, 0)
    s_o = mx_kscale(O, 0)
    return {
        "x": (n((G, D, N)) * s_d[:, None]).astype(np.float32),
        "w1": (n((G, D, M)) / np.sqrt(D) / s_d[:, None]).astype(np.float32),
        "w2": (n((G, D, M)) / np.sqrt(D) / s_d[:, None]).astype(np.float32),
        "st": (np.random.uniform(4.0, 16.0, (G, M, 1))).astype(np.float32),
        "gb": (0.5 * n((G, M, 1))).astype(np.float32),
        "wo": (n((G, O, M)) / np.sqrt(O) / s_o[:, None]).astype(np.float32),
        "dy": (n((G, O, N)) * s_o[:, None]).astype(np.float32),
        "old": (0.3 * n((G, M, N))).astype(np.float32),
    }


def reference(x, w1, w2, st, gb, wo, dy, old):
    w1q = mxq(f64(w1), 1, "e4m3")
    xq = mxq(f64(x), 1, "e4m3")
    z1 = w1q.transpose(0, 2, 1) @ xq
    w2q = mxq(f64(w2), 1, "e4m3")
    z2 = w2q.transpose(0, 2, 1) @ xq
    mu = np.mean(z1 * z2, axis=-1, keepdims=True)
    gt = sigmoid(mu * f64(st) + f64(gb))
    woq = mxq(f64(wo), 1, "e4m3")
    dyq = mxq(f64(dy), 1, "e4m3")
    c0 = woq.transpose(0, 2, 1) @ dyq
    dgt = np.sum(c0 * z1, axis=-1, keepdims=True)
    dmu = dgt * gt * (1.0 - gt) * f64(st)
    dz1 = c0 * gt + dmu / 512.0 * z2
    y = dz1 + f64(old)
    return y

@@ -1,0 +1,188 @@
+from contextlib import ExitStack
+
+import concourse.mybir as mybir
+
+G, D, M, N = 4, 128, 128, 512
+FLOPS = 3 * 2 * G * D * M * N
+
+F32 = mybir.dt.float32
+BF16 = mybir.dt.bfloat16
+U32 = mybir.dt.uint32
+U8 = mybir.dt.uint8
+FP8X4 = mybir.dt.float8_e4m3fn_x4
+ALU = mybir.AluOpType
+ACT = mybir.ActivationFunctionType
+
+P = 128
+PACK = 4
+ROWS = D // PACK
+HALF = N // 2
+MM = 128
+
+
+def tile_rows_browgate_kernel(tc, x, w1, w2, st, gb, wo, dy, old, out):
+    nc = tc.nc
+    with ExitStack() as ctx:
+        sb = ctx.enter_context(tc.tile_pool(name="sb", bufs=1))
+        ps = ctx.enter_context(tc.psum_pool(name="ps", bufs=1))
+        ctx.enter_context(tc.manual_schedule())
+
+        def operand(name, width):
+            raw = sb.tile([P, PACK, width], F32, name=name + "_raw", align_bytes=64)
+            grouped = sb.tile([P, width, PACK], BF16, name=name + "_bf", align_bytes=64)
+            codes = sb.tile([P, width], U32, name=name + "_codes", align_bytes=64)
+            scales = sb.tile([P, width], U8, name=name + "_scales", align_bytes=64)
+            return {"raw": raw, "grouped": grouped, "codes": codes, "scales": scales}
+
+        def load(op, src, c0, c1):
+            nc.sync.dma_start(out=op["raw"][:], in_=src.rearrange("g (p j) n -> (g p) j n", j=PACK)[:, :, c0:c1])
+
+        def interleave(eng, op, c0, c1):
+            dst = op["grouped"][:, c0:c1, :].rearrange("p (c i) j -> p c j i", i=4)
+            src = op["raw"][:, :, c0:c1].rearrange("p j (c i) -> p c j i", i=4)
+            if eng == "v":
+                nc.vector.tensor_copy(out=dst, in_=src)
+            elif eng == "s":
+                nc.scalar.copy(out=dst, in_=src)
+            else:
+                nc.gpsimd.tensor_scalar(out=op["grouped"][:, c0:c1, :], in0=op["raw"][:, :, c0:c1].rearrange("p j n -> p n j"), scalar1=1.0, scalar2=0.0, op0=ALU.mult, op1=ALU.add)
+
+        def quantize(op):
+            nc.vector.quantize_mx(out=op["codes"][:].bitcast(FP8X4), scales=op["scales"][:],
+                                  in_=op["grouped"][:].rearrange("p n j -> p (n j)"))
+
+        def products(banks, w, mov, h):
+            for c in range(0, HALF, MM):
+                for g in range(G):
+                    r = slice(ROWS * g, ROWS * (g + 1))
+                    nc.tensor.matmul_mx(
+                        out=banks[g][:, h * HALF + c:h * HALF + c + MM],
+                        lhsT=w["codes"][r, :].bitcast(FP8X4), lhsT_scale=w["scales"][r, :],
+                        rhs=mov["codes"][r, c:c + MM].bitcast(FP8X4), rhs_scale=mov["scales"][r, c:c + MM],
+                        start=True, stop=True)
+
+        w1q, w2q, woq = operand("w1", M), operand("w2", M), operand("wo", M)
+        xq = [operand("x%d" % h, HALF) for h in range(2)]
+        dq = [operand("dy%d" % h, HALF) for h in range(2)]
+        bank_a = [ps.tile([P, N], F32, name="a%d" % g) for g in range(G)]
+        bank_b = [ps.tile([P, N], F32, name="b%d" % g) for g in range(G)]
+        z1 = [sb.tile([P, N], F32, name="z1_%d" % g) for g in range(G)]
+        olds = [sb.tile([P, N], F32, name="old%d" % g) for g in range(G)]
+        gated = [sb.tile([P, N], F32, name="gated%d" % g) for g in range(G)]
+        part = [sb.tile([P, N], F32, name="part%d" % g) for g in range(G)]
+        res = [sb.tile([P, N], F32, name="res%d" % g) for g in range(G)]
+        prod = [sb.tile([P, N], F32, name="prod%d" % i) for i in range(2)]
+        rows = sb.tile([P, P], F32, name="rows", align_bytes=64)
+        cols = sb.tile([P, P], F32, name="cols", align_bytes=64)
+        stn = sb.tile([P, G], F32, name="stn")
+        m0 = sb.tile([P, G], F32, name="m0")
+        m1 = sb.tile([P, G], F32, name="m1")
+        bias = sb.tile([P, G], F32, name="bias")
+        nbias = sb.tile([P, G], F32, name="nbias")
+        gate = sb.tile([P, G], F32, name="gate")
+        cogate = sb.tile([P, G], F32, name="cogate")
+        slope = sb.tile([P, G], F32, name="slope")
+        kk = sb.tile([P, G], F32, name="kk")
+        warm = sb.tile([P, 2], F32, name="warm")
+
+        def copy_z1(g, h):
+            c = slice(h * HALF, (h + 1) * HALF)
+            nc.scalar.copy(out=z1[g][:, c], in_=bank_a[g][:, c])
+
+        def mean_part(g, h):
+            c = slice(h * HALF, (h + 1) * HALF)
+            m = (m0, m1)[h]
+            nc.vector.scalar_tensor_tensor(out=prod[g % 2][:, c], in0=bank_b[g][:, c], scalar=stn[:, g:g + 1], in1=z1[g][:, c],
+                                           op0=ALU.mult, op1=ALU.mult, accum_out=m[:, g:g + 1])
+
+        def gates(g):
+            c = slice(g, g + 1)
+            nc.scalar.activation(out=gate[:, c], in_=m1[:, c], func=ACT.Sigmoid, bias=bias[:, c], scale=1.0)
+            nc.scalar.activation(out=cogate[:, c], in_=m1[:, c], func=ACT.Sigmoid, bias=nbias[:, c], scale=-1.0)
+
+        def slopes(g):
+            c = slice(g, g + 1)
+            nc.gpsimd.tensor_scalar(out=slope[:, c], in0=gate[:, c], scalar1=cogate[:, c], scalar2=stn[:, c], op0=ALU.mult, op1=ALU.mult)
+
+        def gate_c0(g):
+            nc.scalar.activation(out=gated[g][:], in_=bank_a[g][:], func=ACT.Copy, scale=gate[:, g:g + 1])
+
+        def add_old(g):
+            nc.gpsimd.tensor_tensor(out=part[g][:], in0=gated[g][:], in1=olds[g][:], op=ALU.add)
+
+        def dgate(g):
+            nc.vector.scalar_tensor_tensor(out=prod[g % 2][:], in0=bank_a[g][:], scalar=slope[:, g:g + 1], in1=z1[g][:],
+                                           op0=ALU.mult, op1=ALU.mult, accum_out=kk[:, g:g + 1])
+
+        def finish(g):
+            nc.vector.scalar_tensor_tensor(out=res[g][:], in0=bank_b[g][:], scalar=kk[:, g:g + 1], in1=part[g][:],
+                                           op0=ALU.mult, op1=ALU.add)
+            nc.sync.dma_start(out=out[g], in_=res[g][:])
+
+        nc.gpsimd.memset(rows[:], 0.0)
+        nc.vector.memset(warm[:, 0:1], 0.0)
+        load(w1q, w1, 0, M)
+        load(xq[0], x, 0, HALF)
+        nc.scalar.dma_start(out=rows[0:P:ROWS, :].rearrange("q (g i) -> q g i", g=G), in_=st.rearrange("g (q i) o -> q g (i o)", q=G))
+        nc.scalar.dma_start(out=rows[1:P:ROWS, :].rearrange("q (g i) -> q g i", g=G), in_=gb.rearrange("g (q i) o -> q g (i o)", q=G))
+        load(w2q, w2, 0, M)
+        load(xq[1], x, HALF, N)
+        load(woq, wo, 0, M)
+        load(dq[0], dy, 0, HALF)
+        load(dq[1], dy, HALF, N)
+        for g in range(G):
+            nc.sync.dma_start(out=olds[g][:], in_=old[g])
+        nc.scalar.activation(out=warm[:, 1:2], in_=warm[:, 0:1], func=ACT.Sigmoid)
+
+        interleave("v", w1q, 0, M)
+        nc.vector.transpose(out=cols[:], in_=rows[:])
+        quantize(w1q)
+        by_group = cols[:].rearrange("p (g r) -> p g r", g=G)
+        nc.gpsimd.tensor_scalar(out=stn[:], in0=by_group[:, :, 0], scalar1=1.0 / N, scalar2=0.0, op0=ALU.mult, op1=ALU.add)
+        interleave("v", xq[0], 0, 176)
+        interleave("s", xq[0], 176, HALF)
+        quantize(xq[0])
+        interleave("s", w2q, 0, M)
+        products(bank_a, w1q, xq[0], 0)
+        quantize(w2q)
+        products(bank_b, w2q, xq[0], 0)
+        copy_z1(0, 0)
+        copy_z1(1, 0)
+        interleave("g", xq[1], 0, 128)
+        interleave("s", xq[1], 128, HALF)
+        interleave("g", woq, 0, M)
+        mean_part(0, 0)
+        mean_part(1, 0)
+        quantize(xq[1])
+        copy_z1(2, 0)
+        copy_z1(3, 0)
+        mean_part(2, 0)
+        mean_part(3, 0)
+        products(bank_a, w1q, xq[1], 1)
+        products(bank_b, w2q, xq[1], 1)
+        quantize(woq)
+        nc.gpsimd.tensor_tensor(out=bias[:], in0=m0[:], in1=by_group[:, :, 1], op=ALU.add)
+        nc.gpsimd.tensor_scalar(out=nbias[:], in0=bias[:], scalar1=-1.0, scalar2=0.0, op0=ALU.mult, op1=ALU.add)
+        interleave("g", dq[0], 0, HALF)
+        for g in range(G):
+            copy_z1(g, 1)
+        interleave("g", dq[1], 0, 128)
+        interleave("s", dq[1], 128, HALF)
+        mean_part(0, 1)
+        mean_part(1, 1)
+        mean_part(2, 1)
+        quantize(dq[0])
+        products(bank_a, woq, dq[0], 0)
+        quantize(dq[1])
+        products(bank_a, woq, dq[1], 1)
+        mean_part(3, 1)
+        for g in range(G):
+            gates(g)
+            slopes(g)
+        for g in range(G):
+            gate_c0(g) if g < 2 else None
+            dgate((g + 2) % G)
+            gate_c0(g) if g >= 2 else None
+            add_old(g)
+        for g in range(G):
+            finish(g)

@@ -27,43 +27,46 @@ def tile_rows_browgate_kernel(tc, x, w1, w2, st, gb, wo, dy, old, out):
         ps = ctx.enter_context(tc.psum_pool(name="ps", bufs=1))
         ctx.enter_context(tc.manual_schedule())
 
-        def operand(name, width):
-            raw = sb.tile([P, PACK, width], F32, name=name + "_raw", align_bytes=64)
-            grouped = sb.tile([P, width, PACK], BF16, name=name + "_bf", align_bytes=64)
+        def operand(name, width, pieces):
+            raw = [sb.tile([P, PACK, width // pieces], F32, name="%s_raw%d" % (name, h), align_bytes=64) for h in range(pieces)]
+            grouped = [sb.tile([P, width // pieces, PACK], BF16, name="%s_bf%d" % (name, h), align_bytes=64) for h in range(pieces)]
             codes = sb.tile([P, width], U32, name=name + "_codes", align_bytes=64)
             scales = sb.tile([P, width], U8, name=name + "_scales", align_bytes=64)
-            return {"raw": raw, "grouped": grouped, "codes": codes, "scales": scales}
+            return {"raw": raw, "grouped": grouped, "codes": codes, "scales": scales, "piece": width // pieces}
 
-        def load(op, src, c0, c1):
-            nc.sync.dma_start(out=op["raw"][:], in_=src.rearrange("g (p j) n -> (g p) j n", j=PACK)[:, :, c0:c1])
+        def load(op, src, h):
+            w = op["piece"]
+            nc.sync.dma_start(out=op["raw"][h][:], in_=src.rearrange("g (p j) n -> (g p) j n", j=PACK)[:, :, h * w:(h + 1) * w])
 
-        def interleave(eng, op, c0, c1):
-            dst = op["grouped"][:, c0:c1, :].rearrange("p (c i) j -> p c j i", i=4)
-            src = op["raw"][:, :, c0:c1].rearrange("p j (c i) -> p c j i", i=4)
+        def interleave(eng, op, h, c0, c1):
+            if c0 == c1:
+                return
+            dst = op["grouped"][h][:, c0:c1, :].rearrange("p (c i) j -> p c j i", i=4)
+            src = op["raw"][h][:, :, c0:c1].rearrange("p j (c i) -> p c j i", i=4)
             if eng == "v":
                 nc.vector.tensor_copy(out=dst, in_=src)
             elif eng == "s":
                 nc.scalar.copy(out=dst, in_=src)
             else:
-                nc.gpsimd.tensor_scalar(out=op["grouped"][:, c0:c1, :], in0=op["raw"][:, :, c0:c1].rearrange("p j n -> p n j"), scalar1=1.0, scalar2=0.0, op0=ALU.mult, op1=ALU.add)
+                nc.gpsimd.tensor_scalar(out=op["grouped"][h][:, c0:c1, :], in0=op["raw"][h][:, :, c0:c1].rearrange("p j n -> p n j"),
+                                        scalar1=1.0, scalar2=0.0, op0=ALU.mult, op1=ALU.add)
 
-        def quantize(op):
-            nc.vector.quantize_mx(out=op["codes"][:].bitcast(FP8X4), scales=op["scales"][:],
-                                  in_=op["grouped"][:].rearrange("p n j -> p (n j)"))
+        def quantize(op, h):
+            c = slice(h * op["piece"], (h + 1) * op["piece"])
+            nc.vector.quantize_mx(out=op["codes"][:, c].bitcast(FP8X4), scales=op["scales"][:, c],
+                                  in_=op["grouped"][h][:].rearrange("p n j -> p (n j)"))
 
-        def products(banks, w, mov, h):
-            for c in range(0, HALF, MM):
-                for g in range(G):
-                    r = slice(ROWS * g, ROWS * (g + 1))
-                    nc.tensor.matmul_mx(
-                        out=banks[g][:, h * HALF + c:h * HALF + c + MM],
-                        lhsT=w["codes"][r, :].bitcast(FP8X4), lhsT_scale=w["scales"][r, :],
-                        rhs=mov["codes"][r, c:c + MM].bitcast(FP8X4), rhs_scale=mov["scales"][r, c:c + MM],
-                        start=True, stop=True)
+        def products(banks, w, mov, groups=range(G)):
+            for g in groups:
+                r = slice(ROWS * g, ROWS * (g + 1))
+                nc.tensor.matmul_mx(
+                    out=banks[g][:],
+                    lhsT=w["codes"][r, :].bitcast(FP8X4), lhsT_scale=w["scales"][r, :],
+                    rhs=mov["codes"][r, :].bitcast(FP8X4), rhs_scale=mov["scales"][r, :],
+                    start=True, stop=True)
 
-        w1q, w2q, woq = operand("w1", M), operand("w2", M), operand("wo", M)
-        xq = [operand("x%d" % h, HALF) for h in range(2)]
-        dq = [operand("dy%d" % h, HALF) for h in range(2)]
+        w1q, w2q, woq = operand("w1", M, 1), operand("w2", M, 1), operand("wo", M, 1)
+        xq, dq = operand("x", N, 2), operand("dy", N, 2)
         bank_a = [ps.tile([P, N], F32, name="a%d" % g) for g in range(G)]
         bank_b = [ps.tile([P, N], F32, name="b%d" % g) for g in range(G)]
         z1 = [sb.tile([P, N], F32, name="z1_%d" % g) for g in range(G)]
@@ -75,9 +78,7 @@ def tile_rows_browgate_kernel(tc, x, w1, w2, st, gb, wo, dy, old, out):
         rows = sb.tile([P, P], F32, name="rows", align_bytes=64)
         cols = sb.tile([P, P], F32, name="cols", align_bytes=64)
         stn = sb.tile([P, G], F32, name="stn")
-        m0 = sb.tile([P, G], F32, name="m0")
-        m1 = sb.tile([P, G], F32, name="m1")
-        bias = sb.tile([P, G], F32, name="bias")
+        mean = sb.tile([P, G], F32, name="mean")
         nbias = sb.tile([P, G], F32, name="nbias")
         gate = sb.tile([P, G], F32, name="gate")
         cogate = sb.tile([P, G], F32, name="cogate")
@@ -85,20 +86,17 @@ def tile_rows_browgate_kernel(tc, x, w1, w2, st, gb, wo, dy, old, out):
         kk = sb.tile([P, G], F32, name="kk")
         warm = sb.tile([P, 2], F32, name="warm")
 
-        def copy_z1(g, h):
-            c = slice(h * HALF, (h + 1) * HALF)
-            nc.scalar.copy(out=z1[g][:, c], in_=bank_a[g][:, c])
+        def copy_z1(g):
+            nc.scalar.copy(out=z1[g][:], in_=bank_a[g][:])
 
-        def mean_part(g, h):
-            c = slice(h * HALF, (h + 1) * HALF)
-            m = (m0, m1)[h]
-            nc.vector.scalar_tensor_tensor(out=prod[g % 2][:, c], in0=bank_b[g][:, c], scalar=stn[:, g:g + 1], in1=z1[g][:, c],
-                                           op0=ALU.mult, op1=ALU.mult, accum_out=m[:, g:g + 1])
+        def row_mean(g):
+            nc.vector.scalar_tensor_tensor(out=prod[g % 2][:], in0=bank_b[g][:], scalar=stn[:, g:g + 1], in1=z1[g][:],
+                                           op0=ALU.mult, op1=ALU.mult, accum_out=mean[:, g:g + 1])
 
         def gates(g):
             c = slice(g, g + 1)
-            nc.scalar.activation(out=gate[:, c], in_=m1[:, c], func=ACT.Sigmoid, bias=bias[:, c], scale=1.0)
-            nc.scalar.activation(out=cogate[:, c], in_=m1[:, c], func=ACT.Sigmoid, bias=nbias[:, c], scale=-1.0)
+            nc.scalar.activation(out=gate[:, c], in_=mean[:, c], func=ACT.Sigmoid, bias=cols[:, ROWS * g + 1:ROWS * g + 2], scale=1.0)
+            nc.scalar.activation(out=cogate[:, c], in_=mean[:, c], func=ACT.Sigmoid, bias=nbias[:, c], scale=-1.0)
 
         def slopes(g):
             c = slice(g, g + 1)
@@ -110,79 +108,86 @@ def tile_rows_browgate_kernel(tc, x, w1, w2, st, gb, wo, dy, old, out):
         def add_old(g):
             nc.gpsimd.tensor_tensor(out=part[g][:], in0=gated[g][:], in1=olds[g][:], op=ALU.add)
 
+        def gate_add(g):
+            nc.vector.scalar_tensor_tensor(out=part[g][:], in0=bank_a[g][:], scalar=gate[:, g:g + 1], in1=olds[g][:],
+                                           op0=ALU.mult, op1=ALU.add)
+
         def dgate(g):
             nc.vector.scalar_tensor_tensor(out=prod[g % 2][:], in0=bank_a[g][:], scalar=slope[:, g:g + 1], in1=z1[g][:],
                                            op0=ALU.mult, op1=ALU.mult, accum_out=kk[:, g:g + 1])
 
-        def finish(g):
-            nc.vector.scalar_tensor_tensor(out=res[g][:], in0=bank_b[g][:], scalar=kk[:, g:g + 1], in1=part[g][:],
+        def finish(g, c0=0, c1=N):
+            nc.vector.scalar_tensor_tensor(out=res[g][:, c0:c1], in0=bank_b[g][:, c0:c1], scalar=kk[:, g:g + 1], in1=part[g][:, c0:c1],
                                            op0=ALU.mult, op1=ALU.add)
-            nc.sync.dma_start(out=out[g], in_=res[g][:])
+            nc.sync.dma_start(out=out[g][:, c0:c1], in_=res[g][:, c0:c1])
 
         nc.gpsimd.memset(rows[:], 0.0)
         nc.vector.memset(warm[:, 0:1], 0.0)
-        load(w1q, w1, 0, M)
-        load(xq[0], x, 0, HALF)
-        nc.scalar.dma_start(out=rows[0:P:ROWS, :].rearrange("q (g i) -> q g i", g=G), in_=st.rearrange("g (q i) o -> q g (i o)", q=G))
-        nc.scalar.dma_start(out=rows[1:P:ROWS, :].rearrange("q (g i) -> q g i", g=G), in_=gb.rearrange("g (q i) o -> q g (i o)", q=G))
-        load(w2q, w2, 0, M)
-        load(xq[1], x, HALF, N)
-        load(woq, wo, 0, M)
-        load(dq[0], dy, 0, HALF)
-        load(dq[1], dy, HALF, N)
+        load(w1q, w1, 0)
+        load(xq, x, 0)
+        nc.sync.dma_start(out=rows[0:P:ROWS, :].rearrange("q (g i) -> q g i", g=G), in_=st.rearrange("g (q i) o -> q g (i o)", q=G))
+        nc.sync.dma_start(out=rows[1:P:ROWS, :].rearrange("q (g i) -> q g i", g=G), in_=gb.rearrange("g (q i) o -> q g (i o)", q=G))
+        load(xq, x, 1)
+        load(w2q, w2, 0)
+        load(woq, wo, 0)
+        load(dq, dy, 0)
+        load(dq, dy, 1)
         for g in range(G):
             nc.sync.dma_start(out=olds[g][:], in_=old[g])
         nc.scalar.activation(out=warm[:, 1:2], in_=warm[:, 0:1], func=ACT.Sigmoid)
-
-        interleave("v", w1q, 0, M)
+        interleave("v", w1q, 0, 0, M)
+        quantize(w1q, 0)
+        interleave("v", xq, 0, 0, 176)
+        interleave("s", xq, 0, 176, HALF)
         nc.vector.transpose(out=cols[:], in_=rows[:])
-        quantize(w1q)
+        quantize(xq, 0)
         by_group = cols[:].rearrange("p (g r) -> p g r", g=G)
-        nc.gpsimd.tensor_scalar(out=stn[:], in0=by_group[:, :, 0], scalar1=1.0 / N, scalar2=0.0, op0=ALU.mult, op1=ALU.add)
-        interleave("v", xq[0], 0, 176)
-        interleave("s", xq[0], 176, HALF)
-        quantize(xq[0])
-        interleave("s", w2q, 0, M)
-        products(bank_a, w1q, xq[0], 0)
-        quantize(w2q)
-        products(bank_b, w2q, xq[0], 0)
-        copy_z1(0, 0)
-        copy_z1(1, 0)
-        interleave("g", xq[1], 0, 128)
-        interleave("s", xq[1], 128, HALF)
-        interleave("g", woq, 0, M)
-        mean_part(0, 0)
-        mean_part(1, 0)
-        quantize(xq[1])
-        copy_z1(2, 0)
-        copy_z1(3, 0)
-        mean_part(2, 0)
-        mean_part(3, 0)
-        products(bank_a, w1q, xq[1], 1)
-        products(bank_b, w2q, xq[1], 1)
-        quantize(woq)
-        nc.gpsimd.tensor_tensor(out=bias[:], in0=m0[:], in1=by_group[:, :, 1], op=ALU.add)
-        nc.gpsimd.tensor_scalar(out=nbias[:], in0=bias[:], scalar1=-1.0, scalar2=0.0, op0=ALU.mult, op1=ALU.add)
-        interleave("g", dq[0], 0, HALF)
+        nc.vector.tensor_scalar(out=stn[:], in0=by_group[:, :, 0], scalar1=1.0 / N, scalar2=None, op0=ALU.mult)
+        interleave("v", xq, 1, 0, 176)
+        interleave("s", xq, 1, 176, HALF)
+        nc.vector.tensor_scalar(out=nbias[:], in0=by_group[:, :, 1], scalar1=-1.0, scalar2=None, op0=ALU.mult)
+        interleave("s", w2q, 0, 0, M)
+        quantize(xq, 1)
+        products(bank_a, w1q, xq, [0, 1])
+        interleave("v", woq, 0, 0, M)
+        quantize(w2q, 0)
+        quantize(woq, 0)
+        products(bank_b, w2q, xq, [0])
+        products(bank_a, w1q, xq, [2])
+        products(bank_b, w2q, xq, [1])
+        products(bank_a, w1q, xq, [3])
+        products(bank_b, w2q, xq, [2, 3])
+        interleave("g", dq, 0, 0, 0)
+        copy_z1(0)
+        interleave("v", dq, 0, 0, HALF)
+        copy_z1(1)
+        row_mean(0)
+        copy_z1(2)
+        interleave("g", dq, 1, 0, 96)
+        interleave("s", dq, 1, 96, HALF)
+        row_mean(1)
+        quantize(dq, 0)
+        copy_z1(3)
+        gates(0)
+        gates(1)
+        row_mean(2)
+        quantize(dq, 1)
+        products(bank_a, woq, dq)
+        row_mean(3)
+        gates(2)
+        gates(3)
         for g in range(G):
-            copy_z1(g, 1)
-        interleave("g", dq[1], 0, 128)
-        interleave("s", dq[1], 128, HALF)
-        mean_part(0, 1)
-        mean_part(1, 1)
-        mean_part(2, 1)
-        quantize(dq[0])
-        products(bank_a, woq, dq[0], 0)
-        quantize(dq[1])
-        products(bank_a, woq, dq[1], 1)
-        mean_part(3, 1)
-        for g in range(G):
-            gates(g)
             slopes(g)
-        for g in range(G):
-            gate_c0(g) if g < 2 else None
-            dgate((g + 2) % G)
-            gate_c0(g) if g >= 2 else None
+        gate_add(0)
+        dgate(0)
+        for g in range(1, G):
+            gate_c0(g)
             add_old(g)
-        for g in range(G):
-            finish(g)
+        dgate(1)
+        finish(0)
+        dgate(2)
+        finish(1)
+        finish(2)
+        dgate(3)
+        finish(3, 0, HALF)
+        finish(3, HALF, N)

@@ -27,33 +27,34 @@ def tile_rows_browgate_kernel(tc, x, w1, w2, st, gb, wo, dy, old, out):
         ps = ctx.enter_context(tc.psum_pool(name="ps", bufs=1))
         ctx.enter_context(tc.manual_schedule())
 
-        def operand(name, width, pieces):
-            raw = [sb.tile([P, PACK, width // pieces], F32, name="%s_raw%d" % (name, h), align_bytes=64) for h in range(pieces)]
-            grouped = [sb.tile([P, width // pieces, PACK], BF16, name="%s_bf%d" % (name, h), align_bytes=64) for h in range(pieces)]
+        def operand(name, width, loads, pieces):
+            raw = [sb.tile([P, PACK, b - a], F32, name="%s_raw%d" % (name, a), align_bytes=64) for a, b in loads]
+            grouped = [sb.tile([P, b - a, PACK], BF16, name="%s_bf%d" % (name, a), align_bytes=64) for a, b in pieces]
             codes = sb.tile([P, width], U32, name=name + "_codes", align_bytes=64)
             scales = sb.tile([P, width], U8, name=name + "_scales", align_bytes=64)
-            return {"raw": raw, "grouped": grouped, "codes": codes, "scales": scales, "piece": width // pieces}
+            return {"raw": raw, "grouped": grouped, "codes": codes, "scales": scales, "loads": loads, "pieces": pieces}
 
         def load(op, src, h):
-            w = op["piece"]
-            nc.sync.dma_start(out=op["raw"][h][:], in_=src.rearrange("g (p j) n -> (g p) j n", j=PACK)[:, :, h * w:(h + 1) * w])
+            a, b = op["loads"][h]
+            nc.sync.dma_start(out=op["raw"][h][:], in_=src.rearrange("g (p j) n -> (g p) j n", j=PACK)[:, :, a:b])
 
-        def interleave(eng, op, h, c0, c1):
+        def interleave(eng, op, c0, c1):
             if c0 == c1:
                 return
-            dst = op["grouped"][h][:, c0:c1, :].rearrange("p (c i) j -> p c j i", i=4)
-            src = op["raw"][h][:, :, c0:c1].rearrange("p j (c i) -> p c j i", i=4)
+            raw, r0 = [(t, a) for t, (a, b) in zip(op["raw"], op["loads"]) if a <= c0 and c1 <= b][0]
+            grouped, g0 = [(t, a) for t, (a, b) in zip(op["grouped"], op["pieces"]) if a <= c0 and c1 <= b][0]
+            dst = grouped[:, c0 - g0:c1 - g0, :]
+            src = raw[:, :, c0 - r0:c1 - r0]
             if eng == "v":
-                nc.vector.tensor_copy(out=dst, in_=src)
+                nc.vector.tensor_copy(out=dst.rearrange("p (c i) j -> p c j i", i=4), in_=src.rearrange("p j (c i) -> p c j i", i=4))
             elif eng == "s":
-                nc.scalar.copy(out=dst, in_=src)
+                nc.scalar.copy(out=dst.rearrange("p (c i) j -> p c j i", i=4), in_=src.rearrange("p j (c i) -> p c j i", i=4))
             else:
-                nc.gpsimd.tensor_scalar(out=op["grouped"][h][:, c0:c1, :], in0=op["raw"][h][:, :, c0:c1].rearrange("p j n -> p n j"),
-                                        scalar1=1.0, scalar2=0.0, op0=ALU.mult, op1=ALU.add)
+                nc.gpsimd.tensor_scalar(out=dst, in0=src.rearrange("p j n -> p n j"), scalar1=1.0, scalar2=0.0, op0=ALU.mult, op1=ALU.add)
 
         def quantize(op, h):
-            c = slice(h * op["piece"], (h + 1) * op["piece"])
-            nc.vector.quantize_mx(out=op["codes"][:, c].bitcast(FP8X4), scales=op["scales"][:, c],
+            a, b = op["pieces"][h]
+            nc.vector.quantize_mx(out=op["codes"][:, a:b].bitcast(FP8X4), scales=op["scales"][:, a:b],
                                   in_=op["grouped"][h][:].rearrange("p n j -> p (n j)"))
 
         def products(banks, w, mov, groups=range(G)):
@@ -65,8 +66,8 @@ def tile_rows_browgate_kernel(tc, x, w1, w2, st, gb, wo, dy, old, out):
                     rhs=mov["codes"][r, :].bitcast(FP8X4), rhs_scale=mov["scales"][r, :],
                     start=True, stop=True)
 
-        w1q, w2q, woq = operand("w1", M, 1), operand("w2", M, 1), operand("wo", M, 1)
-        xq, dq = operand("x", N, 2), operand("dy", N, 2)
+        w1q, w2q, woq = [operand(n, M, [(0, M)], [(0, M)]) for n in ("w1", "w2", "wo")]
+        xq, dq = operand("x", N, [(0, 512)], [(0, 256), (256, 512)]), operand("dy", N, [(0, 256), (256, 512)], [(0, 256), (256, 512)])
         bank_a = [ps.tile([P, N], F32, name="a%d" % g) for g in range(G)]
         bank_b = [ps.tile([P, N], F32, name="b%d" % g) for g in range(G)]
         z1 = [sb.tile([P, N], F32, name="z1_%d" % g) for g in range(G)]
@@ -123,66 +124,68 @@ def tile_rows_browgate_kernel(tc, x, w1, w2, st, gb, wo, dy, old, out):
 
         nc.gpsimd.memset(rows[:], 0.0)
         nc.vector.memset(warm[:, 0:1], 0.0)
-        load(w1q, w1, 0)
         load(xq, x, 0)
+        load(w1q, w1, 0)
         nc.sync.dma_start(out=rows[0:P:ROWS, :].rearrange("q (g i) -> q g i", g=G), in_=st.rearrange("g (q i) o -> q g (i o)", q=G))
         nc.sync.dma_start(out=rows[1:P:ROWS, :].rearrange("q (g i) -> q g i", g=G), in_=gb.rearrange("g (q i) o -> q g (i o)", q=G))
-        load(xq, x, 1)
         load(w2q, w2, 0)
-        load(woq, wo, 0)
         load(dq, dy, 0)
         load(dq, dy, 1)
+        load(woq, wo, 0)
         for g in range(G):
             nc.sync.dma_start(out=olds[g][:], in_=old[g])
         nc.scalar.activation(out=warm[:, 1:2], in_=warm[:, 0:1], func=ACT.Sigmoid)
-        interleave("v", w1q, 0, 0, M)
-        quantize(w1q, 0)
-        interleave("v", xq, 0, 0, 176)
-        interleave("s", xq, 0, 176, HALF)
-        nc.vector.transpose(out=cols[:], in_=rows[:])
+        interleave("v", xq, 0, 192)
+        interleave("s", xq, 192, 256)
+        interleave("s", xq, 256, 400)
+        interleave("v", xq, 400, N)
         quantize(xq, 0)
-        by_group = cols[:].rearrange("p (g r) -> p g r", g=G)
-        nc.vector.tensor_scalar(out=stn[:], in0=by_group[:, :, 0], scalar1=1.0 / N, scalar2=None, op0=ALU.mult)
-        interleave("v", xq, 1, 0, 176)
-        interleave("s", xq, 1, 176, HALF)
-        nc.vector.tensor_scalar(out=nbias[:], in0=by_group[:, :, 1], scalar1=-1.0, scalar2=None, op0=ALU.mult)
-        interleave("s", w2q, 0, 0, M)
+        interleave("v", w1q, 0, M)
         quantize(xq, 1)
+        quantize(w1q, 0)
+        interleave("s", w2q, 0, M)
         products(bank_a, w1q, xq, [0, 1])
-        interleave("v", woq, 0, 0, M)
+        nc.vector.transpose(out=cols[:], in_=rows[:])
         quantize(w2q, 0)
-        quantize(woq, 0)
         products(bank_b, w2q, xq, [0])
         products(bank_a, w1q, xq, [2])
         products(bank_b, w2q, xq, [1])
         products(bank_a, w1q, xq, [3])
         products(bank_b, w2q, xq, [2, 3])
-        interleave("g", dq, 0, 0, 0)
+        by_group = cols[:].rearrange("p (g r) -> p g r", g=G)
+        nc.vector.tensor_scalar(out=stn[:], in0=by_group[:, :, 0], scalar1=1.0 / N, scalar2=None, op0=ALU.mult)
+        nc.vector.tensor_scalar(out=nbias[:], in0=by_group[:, :, 1], scalar1=-1.0, scalar2=None, op0=ALU.mult)
+        interleave("v", dq, 0, 256)
         copy_z1(0)
-        interleave("v", dq, 0, 0, HALF)
+        quantize(dq, 0)
         copy_z1(1)
         row_mean(0)
-        copy_z1(2)
-        interleave("g", dq, 1, 0, 96)
-        interleave("s", dq, 1, 96, HALF)
+        interleave("s", dq, 256, N)
         row_mean(1)
-        quantize(dq, 0)
+        interleave("v", woq, 0, M)
+        copy_z1(2)
         copy_z1(3)
         gates(0)
         gates(1)
-        row_mean(2)
         quantize(dq, 1)
+        quantize(woq, 0)
         products(bank_a, woq, dq)
+        row_mean(2)
         row_mean(3)
         gates(2)
-        gates(3)
-        for g in range(G):
-            slopes(g)
+        slopes(0)
+        slopes(1)
+        slopes(2)
         gate_add(0)
         dgate(0)
-        for g in range(1, G):
-            gate_c0(g)
-            add_old(g)
+        gate_c0(1)
+        gates(3)
+        add_old(1)
+        slopes(3)
+        gate_c0(2)
+        add_old(2)
+        gate_c0(3)
+        add_old(3)
         dgate(1)
         finish(0)
         dgate(2)

@@ -19,7 +19,6 @@ ROWS = D // PACK
 HALF = N // 2
 MM = 128
 
-
 def tile_rows_browgate_kernel(tc, x, w1, w2, st, gb, wo, dy, old, out):
     nc = tc.nc
     with ExitStack() as ctx:
@@ -83,15 +82,15 @@ def tile_rows_browgate_kernel(tc, x, w1, w2, st, gb, wo, dy, old, out):
         nbias = sb.tile([P, G], F32, name="nbias")
         gate = sb.tile([P, G], F32, name="gate")
         cogate = sb.tile([P, G], F32, name="cogate")
-        slope = sb.tile([P, G], F32, name="slope")
+        dsum = sb.tile([P, G], F32, name="dsum")
         kk = sb.tile([P, G], F32, name="kk")
         warm = sb.tile([P, 2], F32, name="warm")
 
         def copy_z1(g):
-            nc.scalar.copy(out=z1[g][:], in_=bank_a[g][:])
+            nc.scalar.activation(out=z1[g][:], in_=bank_a[g][:], func=ACT.Copy, scale=stn[:, g:g + 1])
 
         def row_mean(g):
-            nc.vector.scalar_tensor_tensor(out=prod[g % 2][:], in0=bank_b[g][:], scalar=stn[:, g:g + 1], in1=z1[g][:],
+            nc.vector.scalar_tensor_tensor(out=prod[g % 2][:], in0=bank_b[g][:], scalar=1.0, in1=z1[g][:],
                                            op0=ALU.mult, op1=ALU.mult, accum_out=mean[:, g:g + 1])
 
         def gates(g):
@@ -99,23 +98,23 @@ def tile_rows_browgate_kernel(tc, x, w1, w2, st, gb, wo, dy, old, out):
             nc.scalar.activation(out=gate[:, c], in_=mean[:, c], func=ACT.Sigmoid, bias=cols[:, ROWS * g + 1:ROWS * g + 2], scale=1.0)
             nc.scalar.activation(out=cogate[:, c], in_=mean[:, c], func=ACT.Sigmoid, bias=nbias[:, c], scale=-1.0)
 
-        def slopes(g):
+        def factor(g):
             c = slice(g, g + 1)
-            nc.gpsimd.tensor_scalar(out=slope[:, c], in0=gate[:, c], scalar1=cogate[:, c], scalar2=stn[:, c], op0=ALU.mult, op1=ALU.mult)
+            nc.scalar.activation(out=kk[:, c], in_=dsum[:, c], func=ACT.Copy, scale=gate[:, c])
 
-        def gate_c0(g):
-            nc.scalar.activation(out=gated[g][:], in_=bank_a[g][:], func=ACT.Copy, scale=gate[:, g:g + 1])
+        def gate_c0(g, c0=0, c1=N):
+            nc.scalar.activation(out=gated[g][:, c0:c1], in_=bank_a[g][:, c0:c1], func=ACT.Copy, scale=gate[:, g:g + 1])
 
-        def add_old(g):
-            nc.gpsimd.tensor_tensor(out=part[g][:], in0=gated[g][:], in1=olds[g][:], op=ALU.add)
+        def add_old(g, c0=0, c1=N):
+            nc.gpsimd.tensor_tensor(out=part[g][:, c0:c1], in0=gated[g][:, c0:c1], in1=olds[g][:, c0:c1], op=ALU.add)
 
-        def gate_add(g):
-            nc.vector.scalar_tensor_tensor(out=part[g][:], in0=bank_a[g][:], scalar=gate[:, g:g + 1], in1=olds[g][:],
+        def gate_add(g, c0=0, c1=N):
+            nc.vector.scalar_tensor_tensor(out=part[g][:, c0:c1], in0=bank_a[g][:, c0:c1], scalar=gate[:, g:g + 1], in1=olds[g][:, c0:c1],
                                            op0=ALU.mult, op1=ALU.add)
 
         def dgate(g):
-            nc.vector.scalar_tensor_tensor(out=prod[g % 2][:], in0=bank_a[g][:], scalar=slope[:, g:g + 1], in1=z1[g][:],
-                                           op0=ALU.mult, op1=ALU.mult, accum_out=kk[:, g:g + 1])
+            nc.vector.scalar_tensor_tensor(out=prod[g % 2][:], in0=bank_a[g][:], scalar=cogate[:, g:g + 1], in1=z1[g][:],
+                                           op0=ALU.mult, op1=ALU.mult, accum_out=dsum[:, g:g + 1])
 
         def finish(g, c0=0, c1=N):
             nc.vector.scalar_tensor_tensor(out=res[g][:, c0:c1], in0=bank_b[g][:, c0:c1], scalar=kk[:, g:g + 1], in1=part[g][:, c0:c1],
@@ -160,37 +159,40 @@ def tile_rows_browgate_kernel(tc, x, w1, w2, st, gb, wo, dy, old, out):
         quantize(dq, 0)
         copy_z1(1)
         row_mean(0)
-        interleave("s", dq, 256, N)
+        copy_z1(2)
+        interleave("g", dq, 256, 384)
+        interleave("s", dq, 384, N)
         row_mean(1)
         interleave("v", woq, 0, M)
-        copy_z1(2)
-        copy_z1(3)
         gates(0)
-        gates(1)
+
         quantize(dq, 1)
         quantize(woq, 0)
+        copy_z1(3)
         products(bank_a, woq, dq)
+
+        gates(1)
         row_mean(2)
         row_mean(3)
         gates(2)
-        slopes(0)
-        slopes(1)
-        slopes(2)
-        gate_add(0)
-        dgate(0)
-        gate_c0(1)
+        gate_c0(0)
+        add_old(0)
         gates(3)
+        dgate(1)
+        gate_c0(1)
         add_old(1)
-        slopes(3)
         gate_c0(2)
         add_old(2)
-        gate_c0(3)
-        add_old(3)
-        dgate(1)
-        finish(0)
-        dgate(2)
-        finish(1)
-        finish(2)
+        dgate(0)
+        factor(1)
+        factor(0)
+        gate_add(3)
         dgate(3)
-        finish(3, 0, HALF)
-        finish(3, HALF, N)
+        factor(3)
+        finish(0)
+        finish(3)
+        dgate(2)
+        factor(2)
+        finish(1)
+        finish(2, 0, HALF)
+        finish(2, HALF, N)

from contextlib import ExitStack

import concourse.mybir as mybir

G, D, M, N = 4, 128, 128, 512
FLOPS = 3 * 2 * G * D * M * N

F32 = mybir.dt.float32
BF16 = mybir.dt.bfloat16
U32 = mybir.dt.uint32
U8 = mybir.dt.uint8
FP8X4 = mybir.dt.float8_e4m3fn_x4
ALU = mybir.AluOpType
ACT = mybir.ActivationFunctionType

P = 128
PACK = 4
ROWS = D // PACK
HALF = N // 2
MM = 128

def tile_rows_browgate_kernel(tc, x, w1, w2, st, gb, wo, dy, old, out):
    nc = tc.nc
    with ExitStack() as ctx:
        sb = ctx.enter_context(tc.tile_pool(name="sb", bufs=1))
        ps = ctx.enter_context(tc.psum_pool(name="ps", bufs=1))
        ctx.enter_context(tc.manual_schedule())

        def operand(name, width, loads, pieces):
            raw = [sb.tile([P, PACK, b - a], F32, name="%s_raw%d" % (name, a), align_bytes=64) for a, b in loads]
            grouped = [sb.tile([P, b - a, PACK], BF16, name="%s_bf%d" % (name, a), align_bytes=64) for a, b in pieces]
            codes = sb.tile([P, width], U32, name=name + "_codes", align_bytes=64)
            scales = sb.tile([P, width], U8, name=name + "_scales", align_bytes=64)
            return {"raw": raw, "grouped": grouped, "codes": codes, "scales": scales, "loads": loads, "pieces": pieces}

        def load(op, src, h):
            a, b = op["loads"][h]
            nc.sync.dma_start(out=op["raw"][h][:], in_=src.rearrange("g (p j) n -> (g p) j n", j=PACK)[:, :, a:b])

        def interleave(eng, op, c0, c1):
            if c0 == c1:
                return
            raw, r0 = [(t, a) for t, (a, b) in zip(op["raw"], op["loads"]) if a <= c0 and c1 <= b][0]
            grouped, g0 = [(t, a) for t, (a, b) in zip(op["grouped"], op["pieces"]) if a <= c0 and c1 <= b][0]
            dst = grouped[:, c0 - g0:c1 - g0, :]
            src = raw[:, :, c0 - r0:c1 - r0]
            if eng == "v":
                nc.vector.tensor_copy(out=dst.rearrange("p (c i) j -> p c j i", i=4), in_=src.rearrange("p j (c i) -> p c j i", i=4))
            elif eng == "s":
                nc.scalar.copy(out=dst.rearrange("p (c i) j -> p c j i", i=4), in_=src.rearrange("p j (c i) -> p c j i", i=4))
            else:
                nc.gpsimd.tensor_scalar(out=dst, in0=src.rearrange("p j n -> p n j"), scalar1=1.0, scalar2=0.0, op0=ALU.mult, op1=ALU.add)

        def quantize(op, h):
            a, b = op["pieces"][h]
            nc.vector.quantize_mx(out=op["codes"][:, a:b].bitcast(FP8X4), scales=op["scales"][:, a:b],
                                  in_=op["grouped"][h][:].rearrange("p n j -> p (n j)"))

        def products(banks, w, mov, groups=range(G)):
            for g in groups:
                r = slice(ROWS * g, ROWS * (g + 1))
                nc.tensor.matmul_mx(
                    out=banks[g][:],
                    lhsT=w["codes"][r, :].bitcast(FP8X4), lhsT_scale=w["scales"][r, :],
                    rhs=mov["codes"][r, :].bitcast(FP8X4), rhs_scale=mov["scales"][r, :],
                    start=True, stop=True)

        w1q, w2q, woq = [operand(n, M, [(0, M)], [(0, M)]) for n in ("w1", "w2", "wo")]
        xq, dq = operand("x", N, [(0, 512)], [(0, 256), (256, 512)]), operand("dy", N, [(0, 256), (256, 512)], [(0, 256), (256, 512)])
        bank_a = [ps.tile([P, N], F32, name="a%d" % g) for g in range(G)]
        bank_b = [ps.tile([P, N], F32, name="b%d" % g) for g in range(G)]
        z1 = [sb.tile([P, N], F32, name="z1_%d" % g) for g in range(G)]
        olds = [sb.tile([P, N], F32, name="old%d" % g) for g in range(G)]
        gated = [sb.tile([P, N], F32, name="gated%d" % g) for g in range(G)]
        part = [sb.tile([P, N], F32, name="part%d" % g) for g in range(G)]
        res = [sb.tile([P, N], F32, name="res%d" % g) for g in range(G)]
        prod = [sb.tile([P, N], F32, name="prod%d" % i) for i in range(2)]
        rows = sb.tile([P, P], F32, name="rows", align_bytes=64)
        cols = sb.tile([P, P], F32, name="cols", align_bytes=64)
        stn = sb.tile([P, G], F32, name="stn")
        mean = sb.tile([P, G], F32, name="mean")
        nbias = sb.tile([P, G], F32, name="nbias")
        gate = sb.tile([P, G], F32, name="gate")
        cogate = sb.tile([P, G], F32, name="cogate")
        dsum = sb.tile([P, G], F32, name="dsum")
        kk = sb.tile([P, G], F32, name="kk")
        warm = sb.tile([P, 2], F32, name="warm")

        def copy_z1(g):
            nc.scalar.activation(out=z1[g][:], in_=bank_a[g][:], func=ACT.Copy, scale=stn[:, g:g + 1])

        def row_mean(g):
            nc.vector.scalar_tensor_tensor(out=prod[g % 2][:], in0=bank_b[g][:], scalar=1.0, in1=z1[g][:],
                                           op0=ALU.mult, op1=ALU.mult, accum_out=mean[:, g:g + 1])

        def gates(g):
            c = slice(g, g + 1)
            nc.scalar.activation(out=gate[:, c], in_=mean[:, c], func=ACT.Sigmoid, bias=cols[:, ROWS * g + 1:ROWS * g + 2], scale=1.0)
            nc.scalar.activation(out=cogate[:, c], in_=mean[:, c], func=ACT.Sigmoid, bias=nbias[:, c], scale=-1.0)

        def factor(g):
            c = slice(g, g + 1)
            nc.scalar.activation(out=kk[:, c], in_=dsum[:, c], func=ACT.Copy, scale=gate[:, c])

        def gate_c0(g, c0=0, c1=N):
            nc.scalar.activation(out=gated[g][:, c0:c1], in_=bank_a[g][:, c0:c1], func=ACT.Copy, scale=gate[:, g:g + 1])

        def add_old(g, c0=0, c1=N):
            nc.gpsimd.tensor_tensor(out=part[g][:, c0:c1], in0=gated[g][:, c0:c1], in1=olds[g][:, c0:c1], op=ALU.add)

        def gate_add(g, c0=0, c1=N):
            nc.vector.scalar_tensor_tensor(out=part[g][:, c0:c1], in0=bank_a[g][:, c0:c1], scalar=gate[:, g:g + 1], in1=olds[g][:, c0:c1],
                                           op0=ALU.mult, op1=ALU.add)

        def dgate(g):
            nc.vector.scalar_tensor_tensor(out=prod[g % 2][:], in0=bank_a[g][:], scalar=cogate[:, g:g + 1], in1=z1[g][:],
                                           op0=ALU.mult, op1=ALU.mult, accum_out=dsum[:, g:g + 1])

        def finish(g, c0=0, c1=N):
            nc.vector.scalar_tensor_tensor(out=res[g][:, c0:c1], in0=bank_b[g][:, c0:c1], scalar=kk[:, g:g + 1], in1=part[g][:, c0:c1],
                                           op0=ALU.mult, op1=ALU.add)
            nc.sync.dma_start(out=out[g][:, c0:c1], in_=res[g][:, c0:c1])

        nc.gpsimd.memset(rows[:], 0.0)
        nc.vector.memset(warm[:, 0:1], 0.0)
        load(xq, x, 0)
        load(w1q, w1, 0)
        nc.sync.dma_start(out=rows[0:P:ROWS, :].rearrange("q (g i) -> q g i", g=G), in_=st.rearrange("g (q i) o -> q g (i o)", q=G))
        nc.sync.dma_start(out=rows[1:P:ROWS, :].rearrange("q (g i) -> q g i", g=G), in_=gb.rearrange("g (q i) o -> q g (i o)", q=G))
        load(w2q, w2, 0)
        load(dq, dy, 0)
        load(dq, dy, 1)
        load(woq, wo, 0)
        for g in range(G):
            nc.sync.dma_start(out=olds[g][:], in_=old[g])
        nc.scalar.activation(out=warm[:, 1:2], in_=warm[:, 0:1], func=ACT.Sigmoid)
        interleave("v", xq, 0, 192)
        interleave("s", xq, 192, 256)
        interleave("s", xq, 256, 400)
        interleave("v", xq, 400, N)
        quantize(xq, 0)
        interleave("v", w1q, 0, M)
        quantize(xq, 1)
        quantize(w1q, 0)
        interleave("s", w2q, 0, M)
        products(bank_a, w1q, xq, [0, 1])
        nc.vector.transpose(out=cols[:], in_=rows[:])
        quantize(w2q, 0)
        products(bank_b, w2q, xq, [0])
        products(bank_a, w1q, xq, [2])
        products(bank_b, w2q, xq, [1])
        products(bank_a, w1q, xq, [3])
        products(bank_b, w2q, xq, [2, 3])
        by_group = cols[:].rearrange("p (g r) -> p g r", g=G)
        nc.vector.tensor_scalar(out=stn[:], in0=by_group[:, :, 0], scalar1=1.0 / N, scalar2=None, op0=ALU.mult)
        nc.vector.tensor_scalar(out=nbias[:], in0=by_group[:, :, 1], scalar1=-1.0, scalar2=None, op0=ALU.mult)
        interleave("v", dq, 0, 256)
        copy_z1(0)
        quantize(dq, 0)
        copy_z1(1)
        row_mean(0)
        copy_z1(2)
        interleave("g", dq, 256, 384)
        interleave("s", dq, 384, N)
        row_mean(1)
        interleave("v", woq, 0, M)
        gates(0)

        quantize(dq, 1)
        quantize(woq, 0)
        copy_z1(3)
        products(bank_a, woq, dq)

        gates(1)
        row_mean(2)
        row_mean(3)
        gates(2)
        gate_c0(0)
        add_old(0)
        gates(3)
        dgate(1)
        gate_c0(1)
        add_old(1)
        gate_c0(2)
        add_old(2)
        dgate(0)
        factor(1)
        factor(0)
        gate_add(3)
        dgate(3)
        factor(3)
        finish(0)
        finish(3)
        dgate(2)
        factor(2)
        finish(1)
        finish(2, 0, HALF)
        finish(2, HALF, N)
